import numpy as np
import ml_dtypes


def mxq(x, axis, fmt="e4m3"):
    dtype, down = {"e4m3": (ml_dtypes.float8_e4m3fn, 7), "e5m2": (ml_dtypes.float8_e5m2, 14)}[fmt]
    v = np.moveaxis(np.asarray(x, np.float32).astype(ml_dtypes.bfloat16).astype(np.float64), axis, -1)
    blocks = v.reshape(v.shape[:-1] + (-1, 32))
    amax = np.abs(blocks).max(-1, keepdims=True)
    byte = np.maximum(np.where(amax > 0, np.frexp(amax)[1] - 1 + 127, 0) - down, 1)
    scale = np.exp2(byte - 127.0)
    codes = (blocks / scale).astype(np.float32).astype(dtype).astype(np.float64)
    return np.moveaxis((codes * scale).reshape(v.shape), -1, axis)


WIDE = False


def mx_kscale(k):
    if not WIDE:
        return np.ones(k)
    levels = np.array([10, -10, 5, -5, 0])
    if k % 512:
        return np.exp2(np.random.permutation(np.resize(levels, k // 32))).repeat(32)
    a = np.empty((k // 512, 16))
    for p in range(k // 512):
        a[p, :8] = np.random.permutation(np.resize(levels, 8))
        for g in range(8):
            far = levels[np.abs(levels - a[p, g]) >= 10]
            a[p, g + 8] = far[np.random.randint(len(far))]
    return np.exp2(a.ravel()).repeat(32)


def f64(x):
    return np.asarray(x).astype(np.float64)


def striped(idx):
    return np.tile(np.asarray(idx).reshape(-1, 16).T, (8, 1)).astype(np.uint16)


def unstriped(offs):
    return offs[:16].T.reshape(-1).astype(np.int64)


def striped8(idx):
    return np.asarray(idx).reshape(8, -1, 16).transpose(0, 2, 1).reshape(128, -1).astype(np.uint16)


def unstriped8(offs):
    return offs.reshape(8, 16, -1).transpose(0, 2, 1).reshape(8, -1).astype(np.int64)


def pick8(x, idx, run):
    r = np.arange(len(x))
    return x[r[:, None], idx[r % (8 * run) // run]]


K, T, I, C, O, U = 512, 1024, 256, 512, 256, 256


def setup_inputs():
    n = np.random.standard_normal
    idx = np.stack([np.random.permutation(T)[:O] for _ in range(8)])
    idx2 = np.random.permutation(C)[:I]
    idx3 = np.random.permutation(C)[:U]
    fk = mx_kscale(K)
    return {
        "ca": (np.random.randint(-7, 8, (K, T)).astype(np.float64)).astype(np.float32),
        "cb": (np.random.randint(-7, 8, (K, I)).astype(np.float64)).astype(np.float32),
        "sa": (np.random.uniform(0.1, 0.4, (K, 1)) * fk[:, None]).astype(np.float32),
        "sb": (np.random.uniform(0.01, 0.04, (K, 1)) / fk[:, None]).astype(np.float32),
        "offs": striped8(idx),
        "offs2": striped(idx2),
        "offs3": striped(idx3),
    }


def reference(ca, cb, sa, sb, offs, offs2, offs3):
    idx = unstriped8(offs)
    idx2 = unstriped(offs2)
    idx3 = unstriped(offs3)
    z1 = pick8(f64(ca), idx, 64) * f64(sa)
    pb = np.zeros((K, C))
    pb[:, idx2] = f64(cb) * f64(sb)
    z2 = pb[:, idx3]
    z1q = mxq(z1, 0, "e4m3")
    z2q = mxq(z2, 0, "e4m3")
    y = z1q.T @ z2q
    return y

@@ -1,0 +1,94 @@
+from contextlib import ExitStack
+
+import concourse.mybir as mybir
+
+K, T, I, C, O, U = 512, 1024, 256, 512, 256, 256
+FLOPS = 2 * K * O * U
+
+F32 = mybir.dt.float32
+BF16 = mybir.dt.bfloat16
+U32 = mybir.dt.uint32
+U16 = mybir.dt.uint16
+U8 = mybir.dt.uint8
+FP8X4 = mybir.dt.float8_e4m3fn_x4
+COPY = mybir.ActivationFunctionType.Copy
+
+P = 128
+PACK = 4
+PER_COL = 16
+M_TILE = 128
+PARTS = (128, 64, 64)
+
+
+def tile_list_boardscores_kernel(tc, ca, cb, sa, sb, offs, offs2, offs3, out):
+    nc = tc.nc
+    with ExitStack() as ctx:
+        lists = ctx.enter_context(tc.tile_pool(name="lists", bufs=1))
+        keep = ctx.enter_context(tc.tile_pool(name="keep", bufs=1))
+        psum = ctx.enter_context(tc.psum_pool(name="psum", bufs=1))
+
+        l1 = lists.tile([P, O // PER_COL], U16, name="l1")
+        l2 = lists.tile([P, I // PER_COL], U16, name="l2")
+        l3 = lists.tile([P, U // PER_COL], U16, name="l3")
+        sa_t = keep.tile([P, PACK], F32, name="sa_t")
+        sb_t = keep.tile([P, PACK], F32, name="sb_t")
+        cb_first = keep.tile([P, I], F32, name="cb_first")
+        cb_rest = keep.tile([P, (PACK - 1) * I], F32, name="cb_rest")
+        tables = [keep.tile([P, T], F32, name="table%d" % r) for r in range(PACK)]
+        boards = [keep.tile([P, C], F32, name="board%d" % r) for r in range(PACK)]
+
+        ca_rows = ca.rearrange("(p r) t -> p r t", r=PACK)
+        cb_rows = cb.rearrange("(p r) i -> p (r i)", r=PACK)
+        nc.sync.dma_start(out=cb_first[:], in_=cb_rows[:, 0:I])
+        nc.sync.dma_start(l2[:], offs2)
+        nc.scalar.dma_start(out=sb_t[:], in_=sb.rearrange("(p r) one -> p (r one)", r=PACK))
+        nc.sync.dma_start(out=cb_rest[:], in_=cb_rows[:, I : PACK * I])
+        nc.sync.dma_start(l1[:], offs)
+        nc.sync.dma_start(out=sa_t[:], in_=sa.rearrange("(p r) one -> p (r one)", r=PACK))
+        for r in range(PACK):
+            nc.sync.dma_start(out=tables[r][:], in_=ca_rows[:, r, :])
+        nc.sync.dma_start(l3[:], offs3)
+
+        for r in range(PACK):
+            nc.vector.memset(boards[r][:], 0.0)
+
+        for r in range(PACK):
+            src = cb_first[:] if r == 0 else cb_rest[:, (r - 1) * I : r * I]
+            nc.scalar.activation(out=boards[r][:].indirect(l2[:]), in_=src, func=COPY, scale=sb_t[:, r : r + 1])
+
+        z1 = keep.tile([P, PACK * O], BF16, name="z1", align_bytes=64)
+        for r in range(PACK):
+            nc.scalar.activation(
+                out=z1[:, r : PACK * O : PACK], in_=tables[r][:].indirect(l1[:]), func=COPY, scale=sa_t[:, r : r + 1]
+            )
+        z1_codes = keep.tile([P, O], U32, name="z1_codes", align_bytes=64)
+        z1_scales = keep.tile([P, O], U8, name="z1_scales", align_bytes=64)
+        nc.vector.quantize_mx(out=z1_codes[:].bitcast(FP8X4), scales=z1_scales[:], in_=z1[:])
+
+        out_rows = out.rearrange("(h p) u -> p h u", p=M_TILE)
+        halves = O // M_TILE
+        u0 = 0
+        for j, n in enumerate(PARTS):
+            z2 = keep.tile([P, PACK * n], BF16, name="z2_%d" % j, align_bytes=64)
+            picks = l3[:, u0 // PER_COL : (u0 + n) // PER_COL]
+            for r in range(PACK):
+                nc.scalar.activation(out=z2[:, r : PACK * n : PACK], in_=boards[r][:].indirect(picks), func=COPY)
+            z2_codes = keep.tile([P, n], U32, name="z2_codes%d" % j, align_bytes=64)
+            z2_scales = keep.tile([P, n], U8, name="z2_scales%d" % j, align_bytes=64)
+            nc.vector.quantize_mx(out=z2_codes[:].bitcast(FP8X4), scales=z2_scales[:], in_=z2[:])
+            acc = psum.tile([M_TILE, halves, n], F32, name="acc%d" % j)
+            for h in range(halves):
+                cols = slice(h * M_TILE, (h + 1) * M_TILE)
+                nc.tensor.matmul_mx(
+                    out=acc[:, h, :],
+                    lhsT=z1_codes[:, cols].bitcast(FP8X4),
+                    lhsT_scale=z1_scales[:, cols],
+                    rhs=z2_codes[:].bitcast(FP8X4),
+                    rhs_scale=z2_scales[:],
+                    start=True,
+                    stop=True,
+                )
+            res = keep.tile([M_TILE, halves, n], F32, name="res%d" % j)
+            nc.vector.tensor_copy(out=res[:], in_=acc[:])
+            nc.sync.dma_start(out=out_rows[:, :, u0 : u0 + n], in_=res[:])
+            u0 = u0 + n

@@ -51,6 +51,10 @@ def tile_list_boardscores_kernel(tc, ca, cb, sa, sb, offs, offs2, offs3, out):
 
         for r in range(PACK):
             nc.vector.memset(boards[r][:], 0.0)
+        warm_in = keep.tile([P, 1], F32, name="warm_in")
+        warm_out = keep.tile([P, 1], F32, name="warm_out")
+        nc.gpsimd.memset(warm_in[:], 0.0)
+        nc.scalar.activation(out=warm_out[:], in_=warm_in[:], func=COPY)
 
         for r in range(PACK):
             src = cb_first[:] if r == 0 else cb_rest[:, (r - 1) * I : r * I]

@@ -14,10 +14,12 @@ FP8X4 = mybir.dt.float8_e4m3fn_x4
 COPY = mybir.ActivationFunctionType.Copy
 
 P = 128
-PACK = 4
+SLOTS = 4
 PER_COL = 16
 M_TILE = 128
-PARTS = (128, 64, 64)
+HALVES = O // M_TILE
+MIN_OFFSETS = 64
+PARTS = (U - 2 * MIN_OFFSETS, MIN_OFFSETS, MIN_OFFSETS)
 
 
 def tile_list_boardscores_kernel(tc, ca, cb, sa, sb, offs, offs2, offs3, out):
@@ -27,72 +29,108 @@ def tile_list_boardscores_kernel(tc, ca, cb, sa, sb, offs, offs2, offs3, out):
         keep = ctx.enter_context(tc.tile_pool(name="keep", bufs=1))
         psum = ctx.enter_context(tc.psum_pool(name="psum", bufs=1))
 
-        l1 = lists.tile([P, O // PER_COL], U16, name="l1")
-        l2 = lists.tile([P, I // PER_COL], U16, name="l2")
-        l3 = lists.tile([P, U // PER_COL], U16, name="l3")
-        sa_t = keep.tile([P, PACK], F32, name="sa_t")
-        sb_t = keep.tile([P, PACK], F32, name="sb_t")
-        cb_first = keep.tile([P, I], F32, name="cb_first")
-        cb_rest = keep.tile([P, (PACK - 1) * I], F32, name="cb_rest")
-        tables = [keep.tile([P, T], F32, name="table%d" % r) for r in range(PACK)]
-        boards = [keep.tile([P, C], F32, name="board%d" % r) for r in range(PACK)]
+        query_list = lists.tile([P, O // PER_COL], U16, name="query_list")
+        put_list = lists.tile([P, I // PER_COL], U16, name="put_list")
+        cand_list = lists.tile([P, U // PER_COL], U16, name="cand_list")
+        table_step = keep.tile([P, SLOTS], F32, name="table_step")
+        code_step = keep.tile([P, SLOTS], F32, name="code_step")
+        cb0_head = keep.tile([P, MIN_OFFSETS], F32, name="cb0_head")
+        cb0_rest = keep.tile([P, I - MIN_OFFSETS], F32, name="cb0_rest")
+        cb1 = keep.tile([P, I], F32, name="cb1")
+        cb23 = keep.tile([P, 2 * I], F32, name="cb23")
+        tables = [keep.tile([P, T], F32, name="table%d" % r) for r in range(SLOTS)]
+        boards = [keep.tile([P, C], F32, name="board%d" % r) for r in range(SLOTS)]
 
-        ca_rows = ca.rearrange("(p r) t -> p r t", r=PACK)
-        cb_rows = cb.rearrange("(p r) i -> p (r i)", r=PACK)
-        nc.sync.dma_start(out=cb_first[:], in_=cb_rows[:, 0:I])
-        nc.sync.dma_start(l2[:], offs2)
-        nc.scalar.dma_start(out=sb_t[:], in_=sb.rearrange("(p r) one -> p (r one)", r=PACK))
-        nc.sync.dma_start(out=cb_rest[:], in_=cb_rows[:, I : PACK * I])
-        nc.sync.dma_start(l1[:], offs)
-        nc.sync.dma_start(out=sa_t[:], in_=sa.rearrange("(p r) one -> p (r one)", r=PACK))
-        for r in range(PACK):
+        ca_rows = ca.rearrange("(p r) t -> p r t", r=SLOTS)
+        cb_rows = cb.rearrange("(p r) i -> p (r i)", r=SLOTS)
+        nc.sync.dma_start(out=code_step[:], in_=sb.rearrange("(p r) one -> p (r one)", r=SLOTS))
+        nc.sync.dma_start(put_list[:], offs2)
+        nc.sync.dma_start(out=cb0_head[:], in_=cb_rows[:, 0:MIN_OFFSETS])
+        nc.sync.dma_start(out=cb1[:], in_=cb_rows[:, I : 2 * I])
+        nc.sync.dma_start(out=cb0_rest[:], in_=cb_rows[:, MIN_OFFSETS:I])
+        nc.sync.dma_start(out=cb23[:], in_=cb_rows[:, 2 * I : SLOTS * I])
+        nc.sync.dma_start(query_list[:], offs)
+        nc.sync.dma_start(out=table_step[:], in_=sa.rearrange("(p r) one -> p (r one)", r=SLOTS))
+        for r in range(SLOTS):
             nc.sync.dma_start(out=tables[r][:], in_=ca_rows[:, r, :])
-        nc.sync.dma_start(l3[:], offs3)
+        nc.sync.dma_start(cand_list[:], offs3)
 
-        for r in range(PACK):
-            nc.vector.memset(boards[r][:], 0.0)
         warm_in = keep.tile([P, 1], F32, name="warm_in")
         warm_out = keep.tile([P, 1], F32, name="warm_out")
-        nc.gpsimd.memset(warm_in[:], 0.0)
+        nc.vector.memset(warm_in[:], 0.0)
         nc.scalar.activation(out=warm_out[:], in_=warm_in[:], func=COPY)
 
-        for r in range(PACK):
-            src = cb_first[:] if r == 0 else cb_rest[:, (r - 1) * I : r * I]
-            nc.scalar.activation(out=boards[r][:].indirect(l2[:]), in_=src, func=COPY, scale=sb_t[:, r : r + 1])
-
-        z1 = keep.tile([P, PACK * O], BF16, name="z1", align_bytes=64)
-        for r in range(PACK):
+        for r in range(SLOTS):
+            nc.vector.memset(boards[r][:], 0.0)
+        head_cols = MIN_OFFSETS // PER_COL
+        for r, cb_piece, places in (
+            (0, cb0_head[:], put_list[:, 0:head_cols]),
+            (1, cb1[:], put_list[:]),
+            (0, cb0_rest[:], put_list[:, head_cols : I // PER_COL]),
+            (2, cb23[:, 0:I], put_list[:]),
+            (3, cb23[:, I : 2 * I], put_list[:]),
+        ):
             nc.scalar.activation(
-                out=z1[:, r : PACK * O : PACK], in_=tables[r][:].indirect(l1[:]), func=COPY, scale=sa_t[:, r : r + 1]
+                out=boards[r][:].indirect(places), in_=cb_piece, func=COPY, scale=code_step[:, r : r + 1]
+            )
+
+        z1 = keep.tile([P, SLOTS * O], BF16, name="z1", align_bytes=64)
+        for r in range(SLOTS):
+            nc.scalar.activation(
+                out=z1[:, r : SLOTS * O : SLOTS],
+                in_=tables[r][:].indirect(query_list[:]),
+                func=COPY,
+                scale=table_step[:, r : r + 1],
             )
         z1_codes = keep.tile([P, O], U32, name="z1_codes", align_bytes=64)
         z1_scales = keep.tile([P, O], U8, name="z1_scales", align_bytes=64)
         nc.vector.quantize_mx(out=z1_codes[:].bitcast(FP8X4), scales=z1_scales[:], in_=z1[:])
 
-        out_rows = out.rearrange("(h p) u -> p h u", p=M_TILE)
-        halves = O // M_TILE
-        u0 = 0
-        for j, n in enumerate(PARTS):
-            z2 = keep.tile([P, PACK * n], BF16, name="z2_%d" % j, align_bytes=64)
-            picks = l3[:, u0 // PER_COL : (u0 + n) // PER_COL]
-            for r in range(PACK):
-                nc.scalar.activation(out=z2[:, r : PACK * n : PACK], in_=boards[r][:].indirect(picks), func=COPY)
-            z2_codes = keep.tile([P, n], U32, name="z2_codes%d" % j, align_bytes=64)
-            z2_scales = keep.tile([P, n], U8, name="z2_scales%d" % j, align_bytes=64)
-            nc.vector.quantize_mx(out=z2_codes[:].bitcast(FP8X4), scales=z2_scales[:], in_=z2[:])
-            acc = psum.tile([M_TILE, halves, n], F32, name="acc%d" % j)
-            for h in range(halves):
-                cols = slice(h * M_TILE, (h + 1) * M_TILE)
+        starts = [sum(PARTS[:j]) for j in range(len(PARTS))]
+        z2_parts = []
+        for j, (u0, width) in enumerate(zip(starts, PARTS)):
+            z2 = keep.tile([P, SLOTS * width], BF16, name="z2_%d" % j, align_bytes=64)
+            picks = cand_list[:, u0 // PER_COL : (u0 + width) // PER_COL]
+            for r in range(SLOTS):
+                nc.scalar.activation(
+                    out=z2[:, r : SLOTS * width : SLOTS], in_=boards[r][:].indirect(picks), func=COPY
+                )
+            z2_parts.append(z2)
+
+        def quantise(j):
+            codes = keep.tile([P, PARTS[j]], U32, name="z2_codes%d" % j, align_bytes=64)
+            scales = keep.tile([P, PARTS[j]], U8, name="z2_scales%d" % j, align_bytes=64)
+            nc.vector.quantize_mx(out=codes[:].bitcast(FP8X4), scales=scales[:], in_=z2_parts[j][:])
+            return codes, scales
+
+        def multiply(sums, codes, scales):
+            for h in range(HALVES):
+                queries = slice(h * M_TILE, (h + 1) * M_TILE)
                 nc.tensor.matmul_mx(
-                    out=acc[:, h, :],
-                    lhsT=z1_codes[:, cols].bitcast(FP8X4),
-                    lhsT_scale=z1_scales[:, cols],
-                    rhs=z2_codes[:].bitcast(FP8X4),
-                    rhs_scale=z2_scales[:],
+                    out=sums[h],
+                    lhsT=z1_codes[:, queries].bitcast(FP8X4),
+                    lhsT_scale=z1_scales[:, queries],
+                    rhs=codes[:].bitcast(FP8X4),
+                    rhs_scale=scales[:],
                     start=True,
                     stop=True,
                 )
-            res = keep.tile([M_TILE, halves, n], F32, name="res%d" % j)
-            nc.vector.tensor_copy(out=res[:], in_=acc[:])
-            nc.sync.dma_start(out=out_rows[:, :, u0 : u0 + n], in_=res[:])
-            u0 = u0 + n
+
+        out_rows = out.rearrange("(h p) u -> p h u", p=M_TILE)
+        last = len(PARTS) - 1
+
+        for j, copy_out in zip(range(last), (nc.vector.tensor_copy, nc.scalar.copy)):
+            codes, scales = quantise(j)
+            bank = psum.tile([M_TILE, HALVES, PARTS[j]], F32, name="bank%d" % j)
+            multiply([bank[:, h, :] for h in range(HALVES)], codes, scales)
+            staged = keep.tile([M_TILE, HALVES, PARTS[j]], F32, name="staged%d" % j)
+            copy_out(out=staged[:], in_=bank[:])
+            nc.sync.dma_start(out=out_rows[:, :, starts[j] : starts[j] + PARTS[j]], in_=staged[:])
+
+        codes, scales = quantise(last)
+        banks = [psum.tile([M_TILE, PARTS[last]], F32, name="last_bank%d" % h) for h in range(HALVES)]
+        multiply([banks[h][:] for h in range(HALVES)], codes, scales)
+        for h, copy_out, queue in ((0, nc.vector.tensor_copy, nc.sync), (1, nc.scalar.copy, nc.scalar)):
+            staged = keep.tile([M_TILE, PARTS[last]], F32, name="last_staged%d" % h)
+            copy_out(out=staged[:], in_=banks[h][:])
+            queue.dma_start(out=out_rows[:, h, starts[last] : U], in_=staged[:])

from contextlib import ExitStack

import concourse.mybir as mybir

K, T, I, C, O, U = 512, 1024, 256, 512, 256, 256
FLOPS = 2 * K * O * U

F32 = mybir.dt.float32
BF16 = mybir.dt.bfloat16
U32 = mybir.dt.uint32
U16 = mybir.dt.uint16
U8 = mybir.dt.uint8
FP8X4 = mybir.dt.float8_e4m3fn_x4
COPY = mybir.ActivationFunctionType.Copy

P = 128
SLOTS = 4
PER_COL = 16
M_TILE = 128
HALVES = O // M_TILE
MIN_OFFSETS = 64
PARTS = (U - 2 * MIN_OFFSETS, MIN_OFFSETS, MIN_OFFSETS)


def tile_list_boardscores_kernel(tc, ca, cb, sa, sb, offs, offs2, offs3, out):
    nc = tc.nc
    with ExitStack() as ctx:
        lists = ctx.enter_context(tc.tile_pool(name="lists", bufs=1))
        keep = ctx.enter_context(tc.tile_pool(name="keep", bufs=1))
        psum = ctx.enter_context(tc.psum_pool(name="psum", bufs=1))

        query_list = lists.tile([P, O // PER_COL], U16, name="query_list")
        put_list = lists.tile([P, I // PER_COL], U16, name="put_list")
        cand_list = lists.tile([P, U // PER_COL], U16, name="cand_list")
        table_step = keep.tile([P, SLOTS], F32, name="table_step")
        code_step = keep.tile([P, SLOTS], F32, name="code_step")
        cb0_head = keep.tile([P, MIN_OFFSETS], F32, name="cb0_head")
        cb0_rest = keep.tile([P, I - MIN_OFFSETS], F32, name="cb0_rest")
        cb1 = keep.tile([P, I], F32, name="cb1")
        cb23 = keep.tile([P, 2 * I], F32, name="cb23")
        tables = [keep.tile([P, T], F32, name="table%d" % r) for r in range(SLOTS)]
        boards = [keep.tile([P, C], F32, name="board%d" % r) for r in range(SLOTS)]

        ca_rows = ca.rearrange("(p r) t -> p r t", r=SLOTS)
        cb_rows = cb.rearrange("(p r) i -> p (r i)", r=SLOTS)
        nc.sync.dma_start(out=code_step[:], in_=sb.rearrange("(p r) one -> p (r one)", r=SLOTS))
        nc.sync.dma_start(put_list[:], offs2)
        nc.sync.dma_start(out=cb0_head[:], in_=cb_rows[:, 0:MIN_OFFSETS])
        nc.sync.dma_start(out=cb1[:], in_=cb_rows[:, I : 2 * I])
        nc.sync.dma_start(out=cb0_rest[:], in_=cb_rows[:, MIN_OFFSETS:I])
        nc.sync.dma_start(out=cb23[:], in_=cb_rows[:, 2 * I : SLOTS * I])
        nc.sync.dma_start(query_list[:], offs)
        nc.sync.dma_start(out=table_step[:], in_=sa.rearrange("(p r) one -> p (r one)", r=SLOTS))
        for r in range(SLOTS):
            nc.sync.dma_start(out=tables[r][:], in_=ca_rows[:, r, :])
        nc.sync.dma_start(cand_list[:], offs3)

        warm_in = keep.tile([P, 1], F32, name="warm_in")
        warm_out = keep.tile([P, 1], F32, name="warm_out")
        nc.vector.memset(warm_in[:], 0.0)
        nc.scalar.activation(out=warm_out[:], in_=warm_in[:], func=COPY)

        for r in range(SLOTS):
            nc.vector.memset(boards[r][:], 0.0)
        head_cols = MIN_OFFSETS // PER_COL
        for r, cb_piece, places in (
            (0, cb0_head[:], put_list[:, 0:head_cols]),
            (1, cb1[:], put_list[:]),
            (0, cb0_rest[:], put_list[:, head_cols : I // PER_COL]),
            (2, cb23[:, 0:I], put_list[:]),
            (3, cb23[:, I : 2 * I], put_list[:]),
        ):
            nc.scalar.activation(
                out=boards[r][:].indirect(places), in_=cb_piece, func=COPY, scale=code_step[:, r : r + 1]
            )

        z1 = keep.tile([P, SLOTS * O], BF16, name="z1", align_bytes=64)
        for r in range(SLOTS):
            nc.scalar.activation(
                out=z1[:, r : SLOTS * O : SLOTS],
                in_=tables[r][:].indirect(query_list[:]),
                func=COPY,
                scale=table_step[:, r : r + 1],
            )
        z1_codes = keep.tile([P, O], U32, name="z1_codes", align_bytes=64)
        z1_scales = keep.tile([P, O], U8, name="z1_scales", align_bytes=64)
        nc.vector.quantize_mx(out=z1_codes[:].bitcast(FP8X4), scales=z1_scales[:], in_=z1[:])

        starts = [sum(PARTS[:j]) for j in range(len(PARTS))]
        z2_parts = []
        for j, (u0, width) in enumerate(zip(starts, PARTS)):
            z2 = keep.tile([P, SLOTS * width], BF16, name="z2_%d" % j, align_bytes=64)
            picks = cand_list[:, u0 // PER_COL : (u0 + width) // PER_COL]
            for r in range(SLOTS):
                nc.scalar.activation(
                    out=z2[:, r : SLOTS * width : SLOTS], in_=boards[r][:].indirect(picks), func=COPY
                )
            z2_parts.append(z2)

        def quantise(j):
            codes = keep.tile([P, PARTS[j]], U32, name="z2_codes%d" % j, align_bytes=64)
            scales = keep.tile([P, PARTS[j]], U8, name="z2_scales%d" % j, align_bytes=64)
            nc.vector.quantize_mx(out=codes[:].bitcast(FP8X4), scales=scales[:], in_=z2_parts[j][:])
            return codes, scales

        def multiply(sums, codes, scales):
            for h in range(HALVES):
                queries = slice(h * M_TILE, (h + 1) * M_TILE)
                nc.tensor.matmul_mx(
                    out=sums[h],
                    lhsT=z1_codes[:, queries].bitcast(FP8X4),
                    lhsT_scale=z1_scales[:, queries],
                    rhs=codes[:].bitcast(FP8X4),
                    rhs_scale=scales[:],
                    start=True,
                    stop=True,
                )

        out_rows = out.rearrange("(h p) u -> p h u", p=M_TILE)
        last = len(PARTS) - 1

        for j, copy_out in zip(range(last), (nc.vector.tensor_copy, nc.scalar.copy)):
            codes, scales = quantise(j)
            bank = psum.tile([M_TILE, HALVES, PARTS[j]], F32, name="bank%d" % j)
            multiply([bank[:, h, :] for h in range(HALVES)], codes, scales)
            staged = keep.tile([M_TILE, HALVES, PARTS[j]], F32, name="staged%d" % j)
            copy_out(out=staged[:], in_=bank[:])
            nc.sync.dma_start(out=out_rows[:, :, starts[j] : starts[j] + PARTS[j]], in_=staged[:])

        codes, scales = quantise(last)
        banks = [psum.tile([M_TILE, PARTS[last]], F32, name="last_bank%d" % h) for h in range(HALVES)]
        multiply([banks[h][:] for h in range(HALVES)], codes, scales)
        for h, copy_out, queue in ((0, nc.vector.tensor_copy, nc.sync), (1, nc.scalar.copy, nc.scalar)):
            staged = keep.tile([M_TILE, PARTS[last]], F32, name="last_staged%d" % h)
            copy_out(out=staged[:], in_=banks[h][:])
            queue.dma_start(out=out_rows[:, h, starts[last] : U], in_=staged[:])
